import numpy as np
import ml_dtypes


def mxq(x, axis, fmt="e4m3"):
    dtype, down = {"e4m3": (ml_dtypes.float8_e4m3fn, 7), "e5m2": (ml_dtypes.float8_e5m2, 14)}[fmt]
    v = np.moveaxis(np.asarray(x, np.float32).astype(ml_dtypes.bfloat16).astype(np.float64), axis, -1)
    blocks = v.reshape(v.shape[:-1] + (-1, 32))
    amax = np.abs(blocks).max(-1, keepdims=True)
    byte = np.maximum(np.where(amax > 0, np.frexp(amax)[1] - 1 + 127, 0) - down, 1)
    scale = np.exp2(byte - 127.0)
    codes = (blocks / scale).astype(np.float32).astype(dtype).astype(np.float64)
    return np.moveaxis((codes * scale).reshape(v.shape), -1, axis)


WIDE = False


def mx_kscale(k):
    if not WIDE:
        return np.ones(k)
    levels = np.array([10, -10, 5, -5, 0])
    if k % 512:
        return np.exp2(np.random.permutation(np.resize(levels, k // 32))).repeat(32)
    a = np.empty((k // 512, 16))
    for p in range(k // 512):
        a[p, :8] = np.random.permutation(np.resize(levels, 8))
        for g in range(8):
            far = levels[np.abs(levels - a[p, g]) >= 10]
            a[p, g + 8] = far[np.random.randint(len(far))]
    return np.exp2(a.ravel()).repeat(32)


BF16 = ml_dtypes.bfloat16


def bf(x):
    return np.asarray(x, np.float32).astype(BF16)


def f64(x):
    return np.asarray(x).astype(np.float64)


E2M1 = np.array([0.0, 0.5, 1.0, 1.5, 2.0, 3.0, 4.0, 6.0, -0.0, -0.5, -1.0, -1.5, -2.0, -3.0, -4.0, -6.0])


def pack_weight(w, fmt):
    k, n = w.shape
    w = f64(bf(w)).reshape(k // 32, 32, n)
    amax = np.abs(w).max(1)
    if fmt == "e4m3":
        byte = np.frexp(amax)[1] - 1 + 127 - 7
    else:
        mant, ex = np.frexp(amax / 6.0)
        byte = np.where(mant > 0.5, ex, ex - 1) + 127
    byte = np.clip(np.where(amax > 0, byte, 1), 1, 254)
    scaled = (w * np.exp2(127.0 - byte)[:, None, :]).reshape(k, n).astype(np.float32)
    by_word = np.ascontiguousarray(scaled.reshape(k // 512, 128, 4, n).transpose(0, 1, 3, 2))
    if fmt == "e4m3":
        words = by_word.astype(ml_dtypes.float8_e4m3fn).view(np.uint8)
    else:
        c = by_word.astype(ml_dtypes.float4_e2m1fn).view(np.uint8) & 0xF
        words = c[..., 0::2] | (c[..., 1::2] << 4)
    return np.ascontiguousarray(words), np.ascontiguousarray(byte.astype(np.uint8).reshape(k // 512, 16, n))


def unpack_weight(words, scales, fmt):
    g, p, n, _ = words.shape
    if fmt == "e4m3":
        vals = np.ascontiguousarray(words).view(ml_dtypes.float8_e4m3fn).astype(np.float64)
    else:
        nib = np.empty((g, p, n, 4), np.uint8)
        nib[..., 0::2] = words & 0xF
        nib[..., 1::2] = words >> 4
        vals = E2M1[nib]
    vals = vals * np.repeat(np.exp2(scales.astype(np.float64) - 127.0), 8, axis=1)[..., None]
    return vals.transpose(0, 1, 3, 2).reshape(g * 512, n)
def pack4(w):
    words, scales = pack_weight(w, "e2m1")
    return words.reshape(words.shape[0], 128, -1), scales


def unpack4(words, scales):
    return unpack_weight(words.reshape(words.shape[0], 128, -1, 2), scales, "e2m1")


E4M3FN = np.array([(-1.0 if i & 128 else 1.0) * ((1.0 + (i & 7) / 8.0) * 2.0 ** (((i >> 3) & 15) - 7) if i & 120 else (i & 7) * 2.0 ** -9) for i in range(256)])


def e4m3fn_bytes(y):
    return np.clip(np.asarray(y, np.float64), -448.0, 448.0).astype(np.float32).astype(ml_dtypes.float8_e4m3fn).view(np.uint8)


def e4m3fn_values(b):
    return E4M3FN[b]


T, D, H, E, F, B = 512, 1536, 16, 128, 2048, 128


def setup_inputs():
    s, t = mx_kscale(D), mx_kscale(F)
    X = np.random.standard_normal((T, D)) * s
    Wg = 2.0 * np.random.standard_normal((D, F)) / np.sqrt(D) / s[:, None]
    X_scale = (np.abs(X).reshape(T, D // B, B).max(axis=2) / 448.0).astype(np.float32)
    Wg_scale = (np.abs(Wg).reshape(D // B, B, F // B, B).max(axis=(1, 3)) / 448.0).astype(np.float32)
    X_bytes = e4m3fn_bytes(X / np.repeat(f64(X_scale), B, axis=1))
    Wg_bytes = e4m3fn_bytes(Wg / np.repeat(np.repeat(f64(Wg_scale), B, axis=0), B, axis=1))
    A = bf(np.random.standard_normal((H, T, E)) * t.reshape(H, 1, E))
    Wo_words, Wo_scales = pack4(np.random.standard_normal((F, D)) / np.sqrt(F) / t[:, None])
    return {"X_bytes": X_bytes, "X_scale": X_scale, "Wg_bytes": Wg_bytes, "Wg_scale": Wg_scale,
            "A": A, "Wo_words": Wo_words, "Wo_scales": Wo_scales}


def reference(X_bytes, X_scale, Wg_bytes, Wg_scale, A, Wo_words, Wo_scales):
    X = e4m3fn_values(X_bytes) * np.repeat(f64(X_scale), B, axis=1)
    Wg = e4m3fn_values(Wg_bytes) * np.repeat(np.repeat(f64(Wg_scale), B, axis=0), B, axis=1)
    z = mxq(X, 1, "e4m3") @ mxq(Wg, 0, "e4m3")
    gate = 1.0 / (1.0 + np.exp(-z))
    a = f64(A).transpose(1, 0, 2).reshape(T, F)
    h = a * gate
    y = mxq(h, 1, "e4m3") @ unpack4(Wo_words, Wo_scales)
    return y

@@ -1,0 +1,364 @@
+from contextlib import ExitStack
+
+import concourse.mybir as mybir
+from concourse.masks import make_identity
+
+F32 = mybir.dt.float32
+BF16 = mybir.dt.bfloat16
+U32 = mybir.dt.uint32
+I32 = mybir.dt.int32
+U8 = mybir.dt.uint8
+F8 = mybir.dt.float8_e4m3fn
+FP8X4 = mybir.dt.float8_e4m3fn_x4
+FP4X4 = mybir.dt.float4_e2m1fn_x4
+MULT = mybir.AluOpType.mult
+COPY = mybir.ActivationFunctionType.Copy
+SIGMOID = mybir.ActivationFunctionType.Sigmoid
+
+P = 128
+T, D, F = 512, 1536, 2048
+FLOPS = 2 * 2 * T * D * F
+NG = D // 512
+NF = F // 512
+NS = T // P
+NN = D // 512
+V_COLS = 0
+S_SLOTS = (1, 3)
+LEAD = 2
+
+
+def tile_sigmoid_gated_attention_output_d4_kernel(tc, X_bytes, X_scale, Wg_bytes, Wg_scale, A, Wo_words, Wo_scales, out):
+    nc = tc.nc
+    with ExitStack() as ctx:
+        keep = ctx.enter_context(tc.tile_pool(name="keep", bufs=1))
+        stage = ctx.enter_context(tc.tile_pool(name="stage", bufs=3))
+        psum = ctx.enter_context(tc.psum_pool(name="psum", bufs=1))
+
+        def bank(i, name):
+            return psum.tile([P, 512], F32, name=name, tag="bank%d" % i)
+
+        xb = [keep.tile([P, D], U8, name="xb%d" % s, align_bytes=64) for s in range(NS)]
+        xw = [keep.tile([P, D], BF16, name="xw%d" % s, align_bytes=64) for s in range(NS)]
+        xi = [keep.tile([P, 2 * 1024], BF16, name="xi%d" % g, align_bytes=64) for g in range(NG)]
+        xq = [keep.tile([P, T], U32, name="xq%d" % g, align_bytes=64) for g in range(NG)]
+        xqs = [keep.tile([P, T], U8, name="xqs%d" % g, align_bytes=64) for g in range(NG)]
+        xs = keep.tile([P, NS, 12], F32, name="xs", align_bytes=64)
+        ws = keep.tile([P, NG, 16], F32, name="ws", align_bytes=64)
+        NC = NF * NG
+        wb = [keep.tile([P, 2048], U8, name="wb%d" % c, align_bytes=64) for c in range(NC)]
+        wq = [keep.tile([P, 512], U32, name="wq%d" % c, align_bytes=64) for c in range(NC)]
+        wqs = [keep.tile([P, 512], U8, name="wqs%d" % c, align_bytes=64) for c in range(NC)]
+        asb = [keep.tile([P, F], BF16, name="asb%d" % s, align_bytes=64) for s in range(NS)]
+        wo = [keep.tile([P, 2 * D], U8, name="wo%d" % g, align_bytes=64) for g in range(NF)]
+        wos = keep.tile([P, NF, D], U8, name="wos", align_bytes=64)
+        sg = [keep.tile([P, 4, T], F32, name="sg%d" % g, align_bytes=64) for g in range(NF)]
+        hq = [keep.tile([P, T], U32, name="hq%d" % g, align_bytes=64) for g in range(NF)]
+        hqs = [keep.tile([P, T], U8, name="hqs%d" % g, align_bytes=64) for g in range(NF)]
+        ident = keep.tile([P, P], F32, name="ident")
+        warm = keep.tile([P, 2], F32, name="warm")
+
+        nc.gpsimd.memset(warm[:], 0.0)
+        make_identity(nc, ident[:])
+        nc.gpsimd.memset(wos[:].rearrange("p g n -> p (g n)").bitcast(I32), 0)
+
+        with tc.manual_schedule():
+            def load_x(s):
+                nc.sync.dma_start(out=xb[s][:], in_=X_bytes[P * s : P * (s + 1), :])
+
+            def load_w(c):
+                G, g = divmod(c, NG)
+                nc.sync.dma_start(
+                    out=wb[c][:].rearrange("p (j n) -> p j n", j=4),
+                    in_=Wg_bytes[512 * g : 512 * (g + 1), 512 * G : 512 * (G + 1)].rearrange("(p j) n -> p j n", j=4),
+                )
+
+            def load_a(s):
+                nc.sync.dma_start(
+                    out=asb[s][:].rearrange("p (c e) -> p c e", c=16),
+                    in_=A[:, P * s : P * (s + 1), :].rearrange("c p e -> p c e"),
+                )
+
+            nc.scalar.activation(out=warm[:, 1:2], in_=warm[:, 0:1], func=SIGMOID)
+            load_x(0)
+            nc.sync.dma_start(out=xs[:], in_=X_scale.rearrange("(s p) j -> p s j", p=P))
+            load_w(0)
+            load_x(1)
+            load_x(2)
+            load_x(3)
+            for q in range(4):
+                nc.sync.dma_start(
+                    out=ws[32 * q : 32 * (q + 1), :, :],
+                    in_=Wg_scale.rearrange("(g q) b -> q g b", q=4)[q].partition_broadcast(32),
+                )
+            load_w(1)
+            for c in range(2, 6):
+                load_w(c)
+            load_a(0)
+            load_a(1)
+            load_w(6)
+            load_w(7)
+            nc.sync.dma_start(out=wo[0][:], in_=Wo_words[0])
+            for q in range(4):
+                nc.sync.dma_start(
+                    out=wos[32 * q : 32 * q + 4, :, :].bitcast(I32),
+                    in_=Wo_scales.rearrange("g (q r) n -> q r g n", r=4)[q].bitcast(I32),
+                )
+            load_w(8)
+            load_w(9)
+            nc.sync.dma_start(out=wo[1][:], in_=Wo_words[1])
+            load_w(10)
+            load_w(11)
+            load_a(2)
+            nc.sync.dma_start(out=wo[2][:], in_=Wo_words[2])
+            nc.sync.dma_start(out=wo[3][:], in_=Wo_words[3])
+            load_a(3)
+
+            ww, wi, z, hi, at, y = {}, {}, {}, {}, {}, {}
+
+            def x_scale(s, js):
+                for j in js:
+                    if s in S_SLOTS:
+                        nc.scalar.activation(
+                            out=xw[s][:, P * j : P * (j + 1)],
+                            in_=xb[s][:, P * j : P * (j + 1)].bitcast(F8),
+                            func=COPY,
+                            scale=xs[:, s, j : j + 1],
+                        )
+                        continue
+                    nc.vector.tensor_scalar(
+                        out=xw[s][:, P * j : P * (j + 1)],
+                        in0=xb[s][:, P * j : P * (j + 1)].bitcast(F8),
+                        scalar1=xs[:, s, j : j + 1],
+                        scalar2=None,
+                        op0=MULT,
+                    )
+
+            xt = {}
+
+            def x_turn(h, g):
+                xt[h, g] = bank(3 * h + g, "xt")
+                for si in range(2):
+                    words = xw[2 * h + si][:].bitcast(F32)
+                    for u in range(2):
+                        nc.tensor.transpose(
+                            xt[h, g][:, 256 * u + P * si : 256 * u + P * (si + 1)],
+                            words[:, 256 * g + u : 256 * (g + 1) : 2],
+                            ident[:],
+                        )
+
+            def x_exit(h, g):
+                nc.scalar.copy(
+                    out=xi[g][:, 1024 * h : 1024 * (h + 1)].bitcast(F32).rearrange("p (r u) -> p r u", u=2),
+                    in_=xt[h, g][:].rearrange("p (u r) -> p r u", u=2),
+                )
+
+            def x_quant(h, g):
+                nc.vector.quantize_mx(
+                    out=xq[g][:, 256 * h : 256 * (h + 1)].bitcast(FP8X4),
+                    scales=xqs[g][:, 256 * h : 256 * (h + 1)],
+                    in_=xi[g][:, 1024 * h : 1024 * (h + 1)],
+                )
+
+            def widen(c):
+                ww[c] = stage.tile([P, 2048], BF16, name="ww", tag="ww", bufs=5, align_bytes=64)
+                nc.scalar.copy(out=ww[c][:, V_COLS:], in_=wb[c][:, V_COLS:].bitcast(F8))
+                if V_COLS:
+                    nc.vector.tensor_copy(out=ww[c][:, :V_COLS], in_=wb[c][:, :V_COLS].bitcast(F8))
+
+            def weave(c, bs):
+                G, g = divmod(c, NG)
+                if c not in wi:
+                    wi[c] = stage.tile([P, 2048], BF16, name="wi", tag="wi", align_bytes=64)
+                dst = wi[c][:].rearrange("p (t m j) -> p m t j", t=4, j=4)
+                src = ww[c][:].rearrange("p (j m t) -> p m t j", j=4, t=4)
+                for b in bs:
+                    nc.vector.tensor_scalar(
+                        out=dst[:, 32 * b : 32 * (b + 1)],
+                        in0=src[:, 32 * b : 32 * (b + 1)],
+                        scalar1=ws[:, g, 4 * G + b : 4 * G + b + 1],
+                        scalar2=None,
+                        op0=MULT,
+                    )
+
+            def w_quant(c):
+                nc.vector.quantize_mx(out=wq[c][:].bitcast(FP8X4), scales=wqs[c][:], in_=wi[c][:])
+
+            def z_pass(c):
+                G, g = divmod(c, NG)
+                for t in range(4):
+                    if g == 0:
+                        z[G, t] = bank(t, "z")
+                    nc.tensor.matmul_mx(
+                        out=z[G, t][:],
+                        lhsT=wq[c][:, P * t : P * (t + 1)].bitcast(FP8X4),
+                        lhsT_scale=wqs[c][:, P * t : P * (t + 1)],
+                        rhs=xq[g][:].bitcast(FP8X4),
+                        rhs_scale=xqs[g][:],
+                        start=(g == 0),
+                        stop=(g == NG - 1),
+                    )
+
+            def sigmoid(G, t, lo=0, hi_=T):
+                nc.scalar.activation(out=sg[G][:, t, lo:hi_], in_=z[G, t][:, lo:hi_], func=SIGMOID)
+
+            def a_turn(i, keys):
+                b = bank(i, "at")
+                for k, (G, s) in enumerate(keys):
+                    words = asb[s][:].bitcast(F32)
+                    for u in range(2):
+                        nc.tensor.transpose(
+                            b[:, 256 * k + P * u : 256 * k + P * (u + 1)],
+                            words[:, 256 * G + u : 256 * (G + 1) : 2],
+                            ident[:],
+                        )
+                    at[G, s] = b[:, 256 * k : 256 * (k + 1)].bitcast(BF16)
+
+            def gate(G, s):
+                hi[G, s] = stage.tile([P, 512], BF16, name="hi", tag="hi", align_bytes=64)
+                nc.vector.tensor_tensor(
+                    out=hi[G, s][:].rearrange("p (r u e) -> p r u e", u=2, e=2),
+                    in0=sg[G][:, :, P * s : P * (s + 1)].rearrange("p (u e) r -> p r u e", u=2),
+                    in1=at[G, s].rearrange("p (u r e) -> p r u e", u=2, e=2),
+                    op=MULT,
+                )
+
+            def h_quant(G, s):
+                nc.vector.quantize_mx(
+                    out=hq[G][:, P * s : P * (s + 1)].bitcast(FP8X4),
+                    scales=hqs[G][:, P * s : P * (s + 1)],
+                    in_=hi[G, s][:],
+                )
+
+            def y_pass(s, n, G):
+                nc.tensor.matmul_mx(
+                    out=y[s, n][:],
+                    lhsT=hq[G][:, P * s : P * (s + 1)].bitcast(FP8X4),
+                    lhsT_scale=hqs[G][:, P * s : P * (s + 1)],
+                    rhs=wo[G][:, 1024 * n : 1024 * (n + 1)].bitcast(FP4X4),
+                    rhs_scale=wos[:, G, 512 * n : 512 * (n + 1)],
+                    start=(G == 0),
+                    stop=(G == NF - 1),
+                )
+
+            def y_out(s, n, on_vector):
+                yo = stage.tile([P, 512], F32, name="yo", tag="yo", bufs=8, align_bytes=64)
+                if on_vector:
+                    nc.vector.tensor_copy(out=yo[:], in_=y[s, n][:])
+                else:
+                    nc.scalar.copy(out=yo[:], in_=y[s, n][:])
+                nc.sync.dma_start(out=out[P * s : P * (s + 1), 512 * n : 512 * (n + 1)], in_=yo[:])
+
+            widen(0)
+            x_scale(0, range(12))
+            x_scale(1, range(12))
+            for g in range(NG):
+                x_turn(0, g)
+            x_scale(2, range(12))
+            widen(1)
+            weave(0, (0, 1, 2, 3))
+            x_scale(3, range(12))
+            widen(2)
+            weave(1, (0, 1))
+            w_quant(0)
+            weave(1, (2, 3))
+            for g in range(NG):
+                x_turn(1, g)
+                x_exit(0, g)
+            widen(3)
+            for g in range(NG):
+                x_exit(1, g)
+            weave(2, (0, 1))
+            w_quant(1)
+            weave(2, (2, 3))
+            for g in range(NG):
+                x_quant(0, g)
+
+            for n in range(NN):
+                y[0, n] = bank(5 + n, "y")
+            for c in range(2, NC):
+                G, g = divmod(c, NG)
+                if c + LEAD < NC:
+                    widen(c + LEAD)
+                if g == 0:
+                    for t in range(4):
+                        sigmoid(G - 1, t)
+                    a_turn(4, [(G - 1, 0), (G - 1, 1)])
+                if g == 1 and 0 < G < NF - 1:
+                    gate(G - 1, 0)
+                    gate(G - 1, 1)
+                if c + 1 < NC:
+                    weave(c + 1, (0, 1))
+                w_quant(c)
+                if c == 2:
+                    for k in range(NG):
+                        x_quant(1, k)
+                    z_pass(0)
+                    z_pass(1)
+                z_pass(c)
+                if g == 1 and 0 < G < NF - 1:
+                    h_quant(G - 1, 0)
+                    h_quant(G - 1, 1)
+                    for n in range(NN):
+                        y_pass(0, n, G - 1)
+                if c + 1 < NC:
+                    weave(c + 1, (2, 3))
+
+            L = NF - 1
+            gate(L - 1, 0)
+            gate(L - 1, 1)
+            h_quant(L - 1, 0)
+            h_quant(L - 1, 1)
+            for lo in (0, 256):
+                for t in range(4):
+                    sigmoid(L, t, lo, lo + 256)
+            a_turn(4, [(L, 0), (L, 1)])
+            for n in range(NN):
+                y_pass(0, n, L - 1)
+            for n in range(NN):
+                y[1, n] = bank(n, "y")
+                for G in range(L):
+                    y_pass(1, n, G)
+            gate(L, 0)
+            gate(L, 1)
+            h_quant(L, 0)
+            h_quant(L, 1)
+            a_turn(3, [(0, 2), (1, 2)])
+            for n in range(NN):
+                y_pass(0, n, L)
+                y_out(0, n, False)
+            a_turn(4, [(2, 2), (3, 2)])
+            for n in range(NN):
+                y_pass(1, n, L)
+                y_out(1, n, False)
+            gate(0, 2)
+            gate(1, 2)
+            h_quant(0, 2)
+            gate(2, 2)
+            h_quant(1, 2)
+            gate(3, 2)
+            h_quant(2, 2)
+            a_turn(3, [(0, 3), (1, 3)])
+            gate(0, 3)
+            h_quant(3, 2)
+            y[2, 0] = bank(5, "y")
+            for G in range(NF):
+                y_pass(2, 0, G)
+            y_out(2, 0, False)
+            a_turn(4, [(2, 3), (3, 3)])
+            gate(1, 3)
+            h_quant(0, 3)
+            gate(2, 3)
+            h_quant(1, 3)
+            gate(3, 3)
+            h_quant(2, 3)
+            for n in (1, 2):
+                y[2, n] = bank(5 + n, "y")
+                for G in range(NF):
+                    y_pass(2, n, G)
+                y_out(2, n, False)
+            h_quant(3, 3)
+            for n in range(NN):
+                y[3, n] = bank(n, "y")
+                for G in range(NF):
+                    y_pass(3, n, G)
+                y_out(3, n, n == 1)

@@ -23,8 +23,12 @@ NF = F // 512
 NS = T // P
 NN = D // 512
 V_COLS = 0
-S_SLOTS = (1, 3)
-LEAD = 2
+S_SLOTS = (3,)
+LEAD = 3
+A0 = 3
+AL = 2
+AN = 6
+SL = 0
 
 
 def tile_sigmoid_gated_attention_output_d4_kernel(tc, X_bytes, X_scale, Wg_bytes, Wg_scale, A, Wo_words, Wo_scales, out):
@@ -45,7 +49,8 @@ def tile_sigmoid_gated_attention_output_d4_kernel(tc, X_bytes, X_scale, Wg_bytes
         xs = keep.tile([P, NS, 12], F32, name="xs", align_bytes=64)
         ws = keep.tile([P, NG, 16], F32, name="ws", align_bytes=64)
         NC = NF * NG
-        wb = [keep.tile([P, 2048], U8, name="wb%d" % c, align_bytes=64) for c in range(NC)]
+        wb = {}
+        ai = [keep.tile([P, NF, 512], BF16, name="ai%d" % s, align_bytes=64) for s in range(NS)]
         wq = [keep.tile([P, 512], U32, name="wq%d" % c, align_bytes=64) for c in range(NC)]
         wqs = [keep.tile([P, 512], U8, name="wqs%d" % c, align_bytes=64) for c in range(NC)]
         asb = [keep.tile([P, F], BF16, name="asb%d" % s, align_bytes=64) for s in range(NS)]
@@ -67,6 +72,7 @@ def tile_sigmoid_gated_attention_output_d4_kernel(tc, X_bytes, X_scale, Wg_bytes
 
             def load_w(c):
                 G, g = divmod(c, NG)
+                wb[c] = stage.tile([P, 2048], U8, name="wb", tag="wb", bufs=8, align_bytes=64)
                 nc.sync.dma_start(
                     out=wb[c][:].rearrange("p (j n) -> p j n", j=4),
                     in_=Wg_bytes[512 * g : 512 * (g + 1), 512 * G : 512 * (G + 1)].rearrange("(p j) n -> p j n", j=4),
@@ -94,9 +100,9 @@ def tile_sigmoid_gated_attention_output_d4_kernel(tc, X_bytes, X_scale, Wg_bytes
             for c in range(2, 6):
                 load_w(c)
             load_a(0)
-            load_a(1)
             load_w(6)
             load_w(7)
+            load_a(1)
             nc.sync.dma_start(out=wo[0][:], in_=Wo_words[0])
             for q in range(4):
                 nc.sync.dma_start(
@@ -160,7 +166,7 @@ def tile_sigmoid_gated_attention_output_d4_kernel(tc, X_bytes, X_scale, Wg_bytes
                 )
 
             def widen(c):
-                ww[c] = stage.tile([P, 2048], BF16, name="ww", tag="ww", bufs=5, align_bytes=64)
+                ww[c] = stage.tile([P, 2048], BF16, name="ww", tag="ww", bufs=4, align_bytes=64)
                 nc.scalar.copy(out=ww[c][:, V_COLS:], in_=wb[c][:, V_COLS:].bitcast(F8))
                 if V_COLS:
                     nc.vector.tensor_copy(out=ww[c][:, :V_COLS], in_=wb[c][:, :V_COLS].bitcast(F8))
@@ -201,24 +207,31 @@ def tile_sigmoid_gated_attention_output_d4_kernel(tc, X_bytes, X_scale, Wg_bytes
             def sigmoid(G, t, lo=0, hi_=T):
                 nc.scalar.activation(out=sg[G][:, t, lo:hi_], in_=z[G, t][:, lo:hi_], func=SIGMOID)
 
-            def a_turn(i, keys):
+            def a_turn(i, s, half):
                 b = bank(i, "at")
-                for k, (G, s) in enumerate(keys):
-                    words = asb[s][:].bitcast(F32)
+                words = asb[s][:].bitcast(F32)
+                for k in range(2):
+                    G = 2 * half + k
                     for u in range(2):
                         nc.tensor.transpose(
                             b[:, 256 * k + P * u : 256 * k + P * (u + 1)],
                             words[:, 256 * G + u : 256 * (G + 1) : 2],
                             ident[:],
                         )
-                    at[G, s] = b[:, 256 * k : 256 * (k + 1)].bitcast(BF16)
+                at[s, half] = b
+
+            def a_exit(s, half):
+                nc.scalar.copy(
+                    out=ai[s][:, 2 * half : 2 * half + 2, :].bitcast(F32).rearrange("p k (r u) -> p k r u", u=2),
+                    in_=at[s, half][:].rearrange("p (k u r) -> p k r u", k=2, u=2),
+                )
 
             def gate(G, s):
                 hi[G, s] = stage.tile([P, 512], BF16, name="hi", tag="hi", align_bytes=64)
                 nc.vector.tensor_tensor(
-                    out=hi[G, s][:].rearrange("p (r u e) -> p r u e", u=2, e=2),
-                    in0=sg[G][:, :, P * s : P * (s + 1)].rearrange("p (u e) r -> p r u e", u=2),
-                    in1=at[G, s].rearrange("p (u r e) -> p r u e", u=2, e=2),
+                    out=hi[G, s][:].rearrange("p (r t) -> p r t", t=4),
+                    in0=sg[G][:, :, P * s : P * (s + 1)].rearrange("p t r -> p r t"),
+                    in1=ai[s][:, G, :].rearrange("p (r t) -> p r t", t=4),
                     op=MULT,
                 )
 
@@ -241,7 +254,7 @@ def tile_sigmoid_gated_attention_output_d4_kernel(tc, X_bytes, X_scale, Wg_bytes
                 )
 
             def y_out(s, n, on_vector):
-                yo = stage.tile([P, 512], F32, name="yo", tag="yo", bufs=8, align_bytes=64)
+                yo = stage.tile([P, 512], F32, name="yo", tag="yo", bufs=6, align_bytes=64)
                 if on_vector:
                     nc.vector.tensor_copy(out=yo[:], in_=y[s, n][:])
                 else:
@@ -273,19 +286,18 @@ def tile_sigmoid_gated_attention_output_d4_kernel(tc, X_bytes, X_scale, Wg_bytes
             for g in range(NG):
                 x_quant(0, g)
 
-            for n in range(NN):
-                y[0, n] = bank(5 + n, "y")
             for c in range(2, NC):
                 G, g = divmod(c, NG)
                 if c + LEAD < NC:
+                    if c == 2:
+                        for k in range(4, 2 + LEAD):
+                            widen(k)
                     widen(c + LEAD)
-                if g == 0:
+                if A0 + AL <= c < A0 + AL + AN:
+                    a_exit(*divmod(c - A0 - AL, 2))
+                if g == SL and G > 0:
                     for t in range(4):
                         sigmoid(G - 1, t)
-                    a_turn(4, [(G - 1, 0), (G - 1, 1)])
-                if g == 1 and 0 < G < NF - 1:
-                    gate(G - 1, 0)
-                    gate(G - 1, 1)
                 if c + 1 < NC:
                     weave(c + 1, (0, 1))
                 w_quant(c)
@@ -294,71 +306,42 @@ def tile_sigmoid_gated_attention_output_d4_kernel(tc, X_bytes, X_scale, Wg_bytes
                         x_quant(1, k)
                     z_pass(0)
                     z_pass(1)
-                z_pass(c)
-                if g == 1 and 0 < G < NF - 1:
-                    h_quant(G - 1, 0)
-                    h_quant(G - 1, 1)
-                    for n in range(NN):
-                        y_pass(0, n, G - 1)
+                    z_pass(2)
+                elif g == SL:
+                    for k in range(c - g, c + 1):
+                        z_pass(k)
+                elif g > SL:
+                    z_pass(c)
+                if A0 <= c < A0 + AN:
+                    s, half = divmod(c - A0, 2)
+                    a_turn(4 + half, s, half)
                 if c + 1 < NC:
                     weave(c + 1, (2, 3))
 
             L = NF - 1
-            gate(L - 1, 0)
-            gate(L - 1, 1)
-            h_quant(L - 1, 0)
-            h_quant(L - 1, 1)
+            order = (6, 7, 0, 1, 2, 3, 4, 5, 6, 7, 0, 1)
+            pend = None
             for lo in (0, 256):
                 for t in range(4):
                     sigmoid(L, t, lo, lo + 256)
-            a_turn(4, [(L, 0), (L, 1)])
-            for n in range(NN):
-                y_pass(0, n, L - 1)
-            for n in range(NN):
-                y[1, n] = bank(n, "y")
-                for G in range(L):
-                    y_pass(1, n, G)
-            gate(L, 0)
-            gate(L, 1)
-            h_quant(L, 0)
-            h_quant(L, 1)
-            a_turn(3, [(0, 2), (1, 2)])
-            for n in range(NN):
-                y_pass(0, n, L)
-                y_out(0, n, False)
-            a_turn(4, [(2, 2), (3, 2)])
-            for n in range(NN):
-                y_pass(1, n, L)
-                y_out(1, n, False)
-            gate(0, 2)
-            gate(1, 2)
-            h_quant(0, 2)
-            gate(2, 2)
-            h_quant(1, 2)
-            gate(3, 2)
-            h_quant(2, 2)
-            a_turn(3, [(0, 3), (1, 3)])
-            gate(0, 3)
-            h_quant(3, 2)
-            y[2, 0] = bank(5, "y")
-            for G in range(NF):
-                y_pass(2, 0, G)
-            y_out(2, 0, False)
-            a_turn(4, [(2, 3), (3, 3)])
-            gate(1, 3)
-            h_quant(0, 3)
-            gate(2, 3)
-            h_quant(1, 3)
-            gate(3, 3)
-            h_quant(2, 3)
-            for n in (1, 2):
-                y[2, n] = bank(5 + n, "y")
+            for k in range(AN, 8):
+                s, half = divmod(k, 2)
+                a_turn(4 + half, s, half)
+                a_exit(s, half)
+            for s in range(NS):
+                for n in range(NN):
+                    y[s, n] = bank(order[3 * s + n], "y")
                 for G in range(NF):
-                    y_pass(2, n, G)
-                y_out(2, n, False)
-            h_quant(3, 3)
+                    gate(G, s)
+                    if pend:
+                        h_quant(*pend)
+                        for n in range(NN):
+                            y_pass(pend[1], n, pend[0])
+                        if pend[0] == L:
+                            for n in range(NN):
+                                y_out(pend[1], n, False)
+                    pend = (G, s)
+            h_quant(*pend)
             for n in range(NN):
-                y[3, n] = bank(n, "y")
-                for G in range(NF):
-                    y_pass(3, n, G)
-                y_out(3, n, n == 1)
+                y_pass(pend[1], n, pend[0])
+                y_out(pend[1], n, n == 1)

@@ -8,9 +8,9 @@ BF16 = mybir.dt.bfloat16
 U32 = mybir.dt.uint32
 I32 = mybir.dt.int32
 U8 = mybir.dt.uint8
-F8 = mybir.dt.float8_e4m3fn
-FP8X4 = mybir.dt.float8_e4m3fn_x4
-FP4X4 = mybir.dt.float4_e2m1fn_x4
+E4M3 = mybir.dt.float8_e4m3fn
+E4M3_X4 = mybir.dt.float8_e4m3fn_x4
+E2M1_X4 = mybir.dt.float4_e2m1fn_x4
 MULT = mybir.AluOpType.mult
 COPY = mybir.ActivationFunctionType.Copy
 SIGMOID = mybir.ActivationFunctionType.Sigmoid
@@ -18,20 +18,28 @@ SIGMOID = mybir.ActivationFunctionType.Sigmoid
 P = 128
 T, D, F = 512, 1536, 2048
 FLOPS = 2 * 2 * T * D * F
-NG = D // 512
-NF = F // 512
+SLOTS = 4
+PASS = P * SLOTS
 NS = T // P
+NG = D // PASS
+NF = F // PASS
 NN = D // 512
-V_COLS = 0
-S_SLOTS = (3,)
+NC = NF * NG
+SCALE_BLOCK = 128
+HEADS = 16
+
+SCALAR_BLOCKS = {1: 8}
 LEAD = 3
-A0 = 3
-AL = 2
-AN = 6
-SL = 0
+
+TURN_A = {4: [(2, 0)], 7: [(2, 1)], 8: [(3, 0)], 11: [(3, 1)]}
+COPY_A = {2: [(0, 0), (0, 1)], 3: [(1, 0)], 6: [(1, 1), (2, 0)], 8: [(2, 1)], 10: [(3, 0)], NC: [(3, 1)]}
+GATES = {7: (0, 0), 8: (1, 0)}
+OUT_BANKS = ((5, 6, 7), (0, 1, 2), (3, 5, 6), (7, 0, 1))
 
 
-def tile_sigmoid_gated_attention_output_d4_kernel(tc, X_bytes, X_scale, Wg_bytes, Wg_scale, A, Wo_words, Wo_scales, out):
+def tile_sigmoid_gated_attention_output_d4_kernel(
+    tc, X_bytes, X_scale, Wg_bytes, Wg_scale, A, Wo_words, Wo_scales, out
+):
     nc = tc.nc
     with ExitStack() as ctx:
         keep = ctx.enter_context(tc.tile_pool(name="keep", bufs=1))
@@ -41,307 +49,314 @@ def tile_sigmoid_gated_attention_output_d4_kernel(tc, X_bytes, X_scale, Wg_bytes
         def bank(i, name):
             return psum.tile([P, 512], F32, name=name, tag="bank%d" % i)
 
-        xb = [keep.tile([P, D], U8, name="xb%d" % s, align_bytes=64) for s in range(NS)]
-        xw = [keep.tile([P, D], BF16, name="xw%d" % s, align_bytes=64) for s in range(NS)]
-        xi = [keep.tile([P, 2 * 1024], BF16, name="xi%d" % g, align_bytes=64) for g in range(NG)]
-        xq = [keep.tile([P, T], U32, name="xq%d" % g, align_bytes=64) for g in range(NG)]
-        xqs = [keep.tile([P, T], U8, name="xqs%d" % g, align_bytes=64) for g in range(NG)]
-        xs = keep.tile([P, NS, 12], F32, name="xs", align_bytes=64)
-        ws = keep.tile([P, NG, 16], F32, name="ws", align_bytes=64)
-        NC = NF * NG
-        wb = {}
-        ai = [keep.tile([P, NF, 512], BF16, name="ai%d" % s, align_bytes=64) for s in range(NS)]
-        wq = [keep.tile([P, 512], U32, name="wq%d" % c, align_bytes=64) for c in range(NC)]
-        wqs = [keep.tile([P, 512], U8, name="wqs%d" % c, align_bytes=64) for c in range(NC)]
-        asb = [keep.tile([P, F], BF16, name="asb%d" % s, align_bytes=64) for s in range(NS)]
-        wo = [keep.tile([P, 2 * D], U8, name="wo%d" % g, align_bytes=64) for g in range(NF)]
-        wos = keep.tile([P, NF, D], U8, name="wos", align_bytes=64)
-        sg = [keep.tile([P, 4, T], F32, name="sg%d" % g, align_bytes=64) for g in range(NF)]
-        hq = [keep.tile([P, T], U32, name="hq%d" % g, align_bytes=64) for g in range(NF)]
-        hqs = [keep.tile([P, T], U8, name="hqs%d" % g, align_bytes=64) for g in range(NF)]
+        def keep_list(count, shape, dtype, name):
+            return [keep.tile(shape, dtype, name="%s%d" % (name, i), align_bytes=64) for i in range(count)]
+
+        x_bytes = keep_list(NS, [P, D], U8, "x_bytes")
+        x_values = keep_list(NS, [P, D], BF16, "x_values")
+        x_words = keep_list(NG, [P, SLOTS * T], BF16, "x_words")
+        x_codes = keep_list(NG, [P, T], U32, "x_codes")
+        x_code_scales = keep_list(NG, [P, T], U8, "x_code_scales")
+        x_scale = keep.tile([P, NS, D // SCALE_BLOCK], F32, name="x_scale", align_bytes=64)
+        w_codes = keep_list(NC, [P, PASS], U32, "w_codes")
+        w_code_scales = keep_list(NC, [P, PASS], U8, "w_code_scales")
+        wg_scale = keep.tile([P, NG, F // SCALE_BLOCK], F32, name="wg_scale", align_bytes=64)
+        a_rows = keep_list(NS, [P, F], BF16, "a_rows")
+        a_turned = keep_list(NS, [P, NF, SLOTS * P], BF16, "a_turned")
+        gate_values = keep_list(NF, [P, SLOTS, T], F32, "gate_values")
+        h_codes = keep_list(NF, [P, T], U32, "h_codes")
+        h_code_scales = keep_list(NF, [P, T], U8, "h_code_scales")
+        wo_codes = keep_list(NF, [P, 2 * D], U8, "wo_codes")
+        wo_code_scales = keep.tile([P, NF, D], U8, name="wo_code_scales", align_bytes=64)
         ident = keep.tile([P, P], F32, name="ident")
         warm = keep.tile([P, 2], F32, name="warm")
 
         nc.gpsimd.memset(warm[:], 0.0)
         make_identity(nc, ident[:])
-        nc.gpsimd.memset(wos[:].rearrange("p g n -> p (g n)").bitcast(I32), 0)
+        nc.gpsimd.memset(wo_code_scales[:].rearrange("p g n -> p (g n)").bitcast(I32), 0)
 
-        with tc.manual_schedule():
-            def load_x(s):
-                nc.sync.dma_start(out=xb[s][:], in_=X_bytes[P * s : P * (s + 1), :])
+        w_bytes = {}
 
-            def load_w(c):
-                G, g = divmod(c, NG)
-                wb[c] = stage.tile([P, 2048], U8, name="wb", tag="wb", bufs=8, align_bytes=64)
-                nc.sync.dma_start(
-                    out=wb[c][:].rearrange("p (j n) -> p j n", j=4),
-                    in_=Wg_bytes[512 * g : 512 * (g + 1), 512 * G : 512 * (G + 1)].rearrange("(p j) n -> p j n", j=4),
-                )
+        def load_x_scale():
+            nc.scalar.dma_start(out=x_scale[:], in_=X_scale.rearrange("(p s) j -> p s j", s=NS))
 
-            def load_a(s):
-                nc.sync.dma_start(
-                    out=asb[s][:].rearrange("p (c e) -> p c e", c=16),
-                    in_=A[:, P * s : P * (s + 1), :].rearrange("c p e -> p c e"),
-                )
+        def load_x(s):
+            nc.sync.dma_start(out=x_bytes[s][:], in_=X_bytes.rearrange("(p s) k -> s p k", s=NS)[s])
 
-            nc.scalar.activation(out=warm[:, 1:2], in_=warm[:, 0:1], func=SIGMOID)
-            load_x(0)
-            nc.sync.dma_start(out=xs[:], in_=X_scale.rearrange("(s p) j -> p s j", p=P))
-            load_w(0)
-            load_x(1)
-            load_x(2)
-            load_x(3)
+        def load_w(c):
+            G, g = divmod(c, NG)
+            w_bytes[c] = stage.tile([P, SLOTS * 512], U8, name="w_bytes", tag="w_bytes", bufs=8, align_bytes=64)
+            nc.sync.dma_start(
+                out=w_bytes[c][:].rearrange("p (j n) -> p j n", j=SLOTS),
+                in_=Wg_bytes[PASS * g : PASS * (g + 1), 512 * G : 512 * (G + 1)].rearrange("(p j) n -> p j n", j=SLOTS),
+            )
+
+        def load_wg_scale():
             for q in range(4):
                 nc.sync.dma_start(
-                    out=ws[32 * q : 32 * (q + 1), :, :],
+                    out=wg_scale[32 * q : 32 * (q + 1), :, :],
                     in_=Wg_scale.rearrange("(g q) b -> q g b", q=4)[q].partition_broadcast(32),
                 )
-            load_w(1)
-            for c in range(2, 6):
-                load_w(c)
-            load_a(0)
-            load_w(6)
-            load_w(7)
-            load_a(1)
-            nc.sync.dma_start(out=wo[0][:], in_=Wo_words[0])
+
+        def load_a(s):
+            nc.sync.dma_start(
+                out=a_rows[s][:].rearrange("p (c e) -> p c e", c=HEADS),
+                in_=A.rearrange("c (p s) e -> s p c e", s=NS)[s],
+            )
+
+        def load_wo(G):
+            nc.sync.dma_start(out=wo_codes[G][:], in_=Wo_words[G])
+
+        def load_wo_scales():
             for q in range(4):
                 nc.sync.dma_start(
-                    out=wos[32 * q : 32 * q + 4, :, :].bitcast(I32),
+                    out=wo_code_scales[32 * q : 32 * q + 4, :, :].bitcast(I32),
                     in_=Wo_scales.rearrange("g (q r) n -> q r g n", r=4)[q].bitcast(I32),
                 )
+
+        x_turned = {}
+
+        def scale_x(s):
+            for j in range(D // SCALE_BLOCK):
+                cols = slice(SCALE_BLOCK * j, SCALE_BLOCK * (j + 1))
+                values = x_values[s][:, cols]
+                codes = x_bytes[s][:, cols].bitcast(E4M3)
+                if j < SCALAR_BLOCKS.get(s, 0):
+                    nc.scalar.activation(out=values, in_=codes, func=COPY, scale=x_scale[:, s, j : j + 1])
+                else:
+                    nc.vector.tensor_scalar(
+                        out=values, in0=codes, scalar1=x_scale[:, s, j : j + 1], scalar2=None, op0=MULT
+                    )
+
+        def transpose_words(dst, rows, group):
+            words = rows.bitcast(F32)
+            for u in range(2):
+                nc.tensor.transpose(dst[u], words[:, 256 * group + u : 256 * (group + 1) : 2], ident[:])
+
+        def turn_x(half):
+            for g in range(NG):
+                x_turned[half, g] = bank(NG * half + g, "x_turned")
+                for i in range(2):
+                    dst = [x_turned[half, g][:, 256 * u + P * i : 256 * u + P * (i + 1)] for u in range(2)]
+                    transpose_words(dst, x_values[2 * half + i][:], g)
+
+        def copy_x(half):
+            for g in range(NG):
+                nc.scalar.copy(
+                    out=x_words[g][:, 1024 * half : 1024 * (half + 1)].bitcast(F32).rearrange("p (r u) -> p r u", u=2),
+                    in_=x_turned[half, g][:].rearrange("p (u r) -> p r u", u=2),
+                )
+
+        def quantize_x(half):
+            for g in range(NG):
+                cols = slice(256 * half, 256 * (half + 1))
+                nc.vector.quantize_mx(
+                    out=x_codes[g][:, cols].bitcast(E4M3_X4),
+                    scales=x_code_scales[g][:, cols],
+                    in_=x_words[g][:, 1024 * half : 1024 * (half + 1)],
+                )
+
+        w_wide, w_words = {}, {}
+
+        def widen(c):
+            w_wide[c] = stage.tile([P, SLOTS * 512], BF16, name="w_wide", tag="w_wide", bufs=6, align_bytes=64)
+            nc.scalar.copy(out=w_wide[c][:], in_=w_bytes[c][:].bitcast(E4M3))
+
+        def weave(c, blocks):
+            G, g = divmod(c, NG)
+            if c not in w_words:
+                w_words[c] = stage.tile([P, SLOTS * 512], BF16, name="w_words", tag="w_words", align_bytes=64)
+            dst = w_words[c][:].rearrange("p (t m j) -> p m j t", t=SLOTS, j=SLOTS)
+            src = w_wide[c][:].rearrange("p (j m t) -> p m j t", j=SLOTS, t=SLOTS)
+            for b in blocks:
+                rows = slice(32 * b, 32 * (b + 1))
+                nc.vector.tensor_scalar(
+                    out=dst[:, rows],
+                    in0=src[:, rows],
+                    scalar1=wg_scale[:, g, 4 * G + b : 4 * G + b + 1],
+                    scalar2=None,
+                    op0=MULT,
+                )
+
+        def quantize_w(c):
+            nc.vector.quantize_mx(out=w_codes[c][:].bitcast(E4M3_X4), scales=w_code_scales[c][:], in_=w_words[c][:])
+
+        z = {}
+
+        def multiply_z(c):
+            G, g = divmod(c, NG)
+            for t in range(SLOTS):
+                if g == 0:
+                    z[G, t] = bank(t, "z")
+                cols = slice(P * t, P * (t + 1))
+                nc.tensor.matmul_mx(
+                    out=z[G, t][:],
+                    lhsT=w_codes[c][:, cols].bitcast(E4M3_X4),
+                    lhsT_scale=w_code_scales[c][:, cols],
+                    rhs=x_codes[g][:].bitcast(E4M3_X4),
+                    rhs_scale=x_code_scales[g][:],
+                    start=(g == 0),
+                    stop=(g == NG - 1),
+                )
+
+        def sigmoid(G, tokens):
+            for t in range(SLOTS):
+                nc.scalar.activation(out=gate_values[G][:, t, tokens], in_=z[G, t][:, tokens], func=SIGMOID)
+
+        a_banks = {}
+
+        def turn_a(i, s, half):
+            a_banks[s, half] = bank(i, "a_bank")
+            for k in range(2):
+                dst = [a_banks[s, half][:, 256 * k + P * u : 256 * k + P * (u + 1)] for u in range(2)]
+                transpose_words(dst, a_rows[s][:], 2 * half + k)
+
+        def copy_a(s, half):
+            nc.scalar.copy(
+                out=a_turned[s][:, 2 * half : 2 * half + 2, :].bitcast(F32).rearrange("p k (r u) -> p k r u", u=2),
+                in_=a_banks[s, half][:].rearrange("p (k u r) -> p k r u", k=2, u=2),
+            )
+
+        h_words, y = {}, {}
+
+        def gate(G, s):
+            h_words[G, s] = stage.tile([P, SLOTS * P], BF16, name="h_words", tag="h_words", align_bytes=64)
+            nc.vector.tensor_tensor(
+                out=h_words[G, s][:].rearrange("p (c i t) -> p c t i", i=4, t=SLOTS),
+                in0=gate_values[G][:, :, P * s : P * (s + 1)].rearrange("p t (c i) -> p c t i", i=4),
+                in1=a_turned[s][:, G, :].rearrange("p (c i t) -> p c t i", i=4, t=SLOTS),
+                op=MULT,
+            )
+
+        def quantize_h(G, s):
+            cols = slice(P * s, P * (s + 1))
+            nc.vector.quantize_mx(
+                out=h_codes[G][:, cols].bitcast(E4M3_X4), scales=h_code_scales[G][:, cols], in_=h_words[G, s][:]
+            )
+
+        def multiply_y(G, s, n):
+            if G == 0:
+                y[s, n] = bank(OUT_BANKS[s][n], "y")
+            cols = slice(P * s, P * (s + 1))
+            nc.tensor.matmul_mx(
+                out=y[s, n][:],
+                lhsT=h_codes[G][:, cols].bitcast(E4M3_X4),
+                lhsT_scale=h_code_scales[G][:, cols],
+                rhs=wo_codes[G][:, 1024 * n : 1024 * (n + 1)].bitcast(E2M1_X4),
+                rhs_scale=wo_code_scales[:, G, 512 * n : 512 * (n + 1)],
+                start=(G == 0),
+                stop=(G == NF - 1),
+            )
+
+        def store_y(s, n, pieces):
+            width = 512 // pieces
+            for lo in range(0, 512, width):
+                y_rows = stage.tile([P, 512], F32, name="y_rows", tag="y_rows", bufs=6, align_bytes=64)
+                nc.scalar.copy(out=y_rows[:, :width], in_=y[s, n][:, lo : lo + width])
+                nc.sync.dma_start(
+                    out=out.rearrange("(p s) n -> s p n", s=NS)[s][:, 512 * n + lo : 512 * n + lo + width],
+                    in_=y_rows[:, :width],
+                )
+
+        def add_to_y(G, s):
+            last_tile = s == NS - 1
+            for n in range(NN - 1 if last_tile else NN):
+                multiply_y(G, s, n)
+                if G == NF - 1:
+                    store_y(s, n, 1)
+            if last_tile and G == NF - 1:
+                for k in range(NF):
+                    multiply_y(k, s, NN - 1)
+                store_y(s, NN - 1, 2)
+
+        with tc.manual_schedule():
+            load_x_scale()
+            nc.scalar.activation(out=warm[:, 1:2], in_=warm[:, 0:1], func=SIGMOID)
+            load_x(1)
+            load_x(0)
+            load_w(0)
+            load_x(3)
+            load_w(1)
+            load_x(2)
+            load_w(2)
+            load_wg_scale()
+            load_a(0)
+            load_w(3)
+            load_w(4)
+            load_a(1)
+            load_w(5)
+            load_w(6)
+            load_w(7)
+            load_a(2)
             load_w(8)
             load_w(9)
-            nc.sync.dma_start(out=wo[1][:], in_=Wo_words[1])
+            load_wo_scales()
+            load_wo(0)
             load_w(10)
-            load_w(11)
-            load_a(2)
-            nc.sync.dma_start(out=wo[2][:], in_=Wo_words[2])
-            nc.sync.dma_start(out=wo[3][:], in_=Wo_words[3])
             load_a(3)
+            load_wo(1)
+            load_w(11)
+            load_wo(2)
+            load_wo(3)
 
-            ww, wi, z, hi, at, y = {}, {}, {}, {}, {}, {}
-
-            def x_scale(s, js):
-                for j in js:
-                    if s in S_SLOTS:
-                        nc.scalar.activation(
-                            out=xw[s][:, P * j : P * (j + 1)],
-                            in_=xb[s][:, P * j : P * (j + 1)].bitcast(F8),
-                            func=COPY,
-                            scale=xs[:, s, j : j + 1],
-                        )
-                        continue
-                    nc.vector.tensor_scalar(
-                        out=xw[s][:, P * j : P * (j + 1)],
-                        in0=xb[s][:, P * j : P * (j + 1)].bitcast(F8),
-                        scalar1=xs[:, s, j : j + 1],
-                        scalar2=None,
-                        op0=MULT,
-                    )
-
-            xt = {}
-
-            def x_turn(h, g):
-                xt[h, g] = bank(3 * h + g, "xt")
-                for si in range(2):
-                    words = xw[2 * h + si][:].bitcast(F32)
-                    for u in range(2):
-                        nc.tensor.transpose(
-                            xt[h, g][:, 256 * u + P * si : 256 * u + P * (si + 1)],
-                            words[:, 256 * g + u : 256 * (g + 1) : 2],
-                            ident[:],
-                        )
-
-            def x_exit(h, g):
-                nc.scalar.copy(
-                    out=xi[g][:, 1024 * h : 1024 * (h + 1)].bitcast(F32).rearrange("p (r u) -> p r u", u=2),
-                    in_=xt[h, g][:].rearrange("p (u r) -> p r u", u=2),
-                )
-
-            def x_quant(h, g):
-                nc.vector.quantize_mx(
-                    out=xq[g][:, 256 * h : 256 * (h + 1)].bitcast(FP8X4),
-                    scales=xqs[g][:, 256 * h : 256 * (h + 1)],
-                    in_=xi[g][:, 1024 * h : 1024 * (h + 1)],
-                )
-
-            def widen(c):
-                ww[c] = stage.tile([P, 2048], BF16, name="ww", tag="ww", bufs=4, align_bytes=64)
-                nc.scalar.copy(out=ww[c][:, V_COLS:], in_=wb[c][:, V_COLS:].bitcast(F8))
-                if V_COLS:
-                    nc.vector.tensor_copy(out=ww[c][:, :V_COLS], in_=wb[c][:, :V_COLS].bitcast(F8))
-
-            def weave(c, bs):
-                G, g = divmod(c, NG)
-                if c not in wi:
-                    wi[c] = stage.tile([P, 2048], BF16, name="wi", tag="wi", align_bytes=64)
-                dst = wi[c][:].rearrange("p (t m j) -> p m t j", t=4, j=4)
-                src = ww[c][:].rearrange("p (j m t) -> p m t j", j=4, t=4)
-                for b in bs:
-                    nc.vector.tensor_scalar(
-                        out=dst[:, 32 * b : 32 * (b + 1)],
-                        in0=src[:, 32 * b : 32 * (b + 1)],
-                        scalar1=ws[:, g, 4 * G + b : 4 * G + b + 1],
-                        scalar2=None,
-                        op0=MULT,
-                    )
-
-            def w_quant(c):
-                nc.vector.quantize_mx(out=wq[c][:].bitcast(FP8X4), scales=wqs[c][:], in_=wi[c][:])
-
-            def z_pass(c):
-                G, g = divmod(c, NG)
-                for t in range(4):
-                    if g == 0:
-                        z[G, t] = bank(t, "z")
-                    nc.tensor.matmul_mx(
-                        out=z[G, t][:],
-                        lhsT=wq[c][:, P * t : P * (t + 1)].bitcast(FP8X4),
-                        lhsT_scale=wqs[c][:, P * t : P * (t + 1)],
-                        rhs=xq[g][:].bitcast(FP8X4),
-                        rhs_scale=xqs[g][:],
-                        start=(g == 0),
-                        stop=(g == NG - 1),
-                    )
-
-            def sigmoid(G, t, lo=0, hi_=T):
-                nc.scalar.activation(out=sg[G][:, t, lo:hi_], in_=z[G, t][:, lo:hi_], func=SIGMOID)
-
-            def a_turn(i, s, half):
-                b = bank(i, "at")
-                words = asb[s][:].bitcast(F32)
-                for k in range(2):
-                    G = 2 * half + k
-                    for u in range(2):
-                        nc.tensor.transpose(
-                            b[:, 256 * k + P * u : 256 * k + P * (u + 1)],
-                            words[:, 256 * G + u : 256 * (G + 1) : 2],
-                            ident[:],
-                        )
-                at[s, half] = b
-
-            def a_exit(s, half):
-                nc.scalar.copy(
-                    out=ai[s][:, 2 * half : 2 * half + 2, :].bitcast(F32).rearrange("p k (r u) -> p k r u", u=2),
-                    in_=at[s, half][:].rearrange("p (k u r) -> p k r u", k=2, u=2),
-                )
-
-            def gate(G, s):
-                hi[G, s] = stage.tile([P, 512], BF16, name="hi", tag="hi", align_bytes=64)
-                nc.vector.tensor_tensor(
-                    out=hi[G, s][:].rearrange("p (r t) -> p r t", t=4),
-                    in0=sg[G][:, :, P * s : P * (s + 1)].rearrange("p t r -> p r t"),
-                    in1=ai[s][:, G, :].rearrange("p (r t) -> p r t", t=4),
-                    op=MULT,
-                )
-
-            def h_quant(G, s):
-                nc.vector.quantize_mx(
-                    out=hq[G][:, P * s : P * (s + 1)].bitcast(FP8X4),
-                    scales=hqs[G][:, P * s : P * (s + 1)],
-                    in_=hi[G, s][:],
-                )
-
-            def y_pass(s, n, G):
-                nc.tensor.matmul_mx(
-                    out=y[s, n][:],
-                    lhsT=hq[G][:, P * s : P * (s + 1)].bitcast(FP8X4),
-                    lhsT_scale=hqs[G][:, P * s : P * (s + 1)],
-                    rhs=wo[G][:, 1024 * n : 1024 * (n + 1)].bitcast(FP4X4),
-                    rhs_scale=wos[:, G, 512 * n : 512 * (n + 1)],
-                    start=(G == 0),
-                    stop=(G == NF - 1),
-                )
-
-            def y_out(s, n, on_vector):
-                yo = stage.tile([P, 512], F32, name="yo", tag="yo", bufs=6, align_bytes=64)
-                if on_vector:
-                    nc.vector.tensor_copy(out=yo[:], in_=y[s, n][:])
-                else:
-                    nc.scalar.copy(out=yo[:], in_=y[s, n][:])
-                nc.sync.dma_start(out=out[P * s : P * (s + 1), 512 * n : 512 * (n + 1)], in_=yo[:])
-
+            scale_x(1)
+            scale_x(0)
+            turn_x(0)
             widen(0)
-            x_scale(0, range(12))
-            x_scale(1, range(12))
-            for g in range(NG):
-                x_turn(0, g)
-            x_scale(2, range(12))
             widen(1)
-            weave(0, (0, 1, 2, 3))
-            x_scale(3, range(12))
-            widen(2)
-            weave(1, (0, 1))
-            w_quant(0)
-            weave(1, (2, 3))
-            for g in range(NG):
-                x_turn(1, g)
-                x_exit(0, g)
-            widen(3)
-            for g in range(NG):
-                x_exit(1, g)
-            weave(2, (0, 1))
-            w_quant(1)
-            weave(2, (2, 3))
-            for g in range(NG):
-                x_quant(0, g)
+            scale_x(3)
+            copy_x(0)
+            scale_x(2)
+            turn_x(1)
+            copy_x(1)
+            weave(0, range(4))
+            weave(1, range(4))
+            turn_a(7, 0, 1)
+            turn_a(6, 0, 0)
+            quantize_x(0)
+            quantize_w(0)
+            quantize_x(1)
+            quantize_w(1)
+            for c in range(2, 2 + LEAD):
+                widen(c)
+            multiply_z(0)
+            turn_a(5, 1, 1)
+            turn_a(4, 1, 0)
+            weave(2, range(4))
+            multiply_z(1)
 
             for c in range(2, NC):
                 G, g = divmod(c, NG)
+                if g == 0:
+                    sigmoid(G - 1, slice(0, T))
                 if c + LEAD < NC:
-                    if c == 2:
-                        for k in range(4, 2 + LEAD):
-                            widen(k)
                     widen(c + LEAD)
-                if A0 + AL <= c < A0 + AL + AN:
-                    a_exit(*divmod(c - A0 - AL, 2))
-                if g == SL and G > 0:
-                    for t in range(4):
-                        sigmoid(G - 1, t)
+                for s, half in COPY_A.get(c, []):
+                    copy_a(s, half)
                 if c + 1 < NC:
                     weave(c + 1, (0, 1))
-                w_quant(c)
-                if c == 2:
-                    for k in range(NG):
-                        x_quant(1, k)
-                    z_pass(0)
-                    z_pass(1)
-                    z_pass(2)
-                elif g == SL:
-                    for k in range(c - g, c + 1):
-                        z_pass(k)
-                elif g > SL:
-                    z_pass(c)
-                if A0 <= c < A0 + AN:
-                    s, half = divmod(c - A0, 2)
-                    a_turn(4 + half, s, half)
+                if c in GATES:
+                    gate(*GATES[c])
+                quantize_w(c)
+                multiply_z(c)
+                for s, half in TURN_A.get(c, []):
+                    turn_a(4, s, half)
                 if c + 1 < NC:
                     weave(c + 1, (2, 3))
+                if c in GATES:
+                    quantize_h(*GATES[c])
+                    add_to_y(*GATES[c])
 
-            L = NF - 1
-            order = (6, 7, 0, 1, 2, 3, 4, 5, 6, 7, 0, 1)
-            pend = None
-            for lo in (0, 256):
-                for t in range(4):
-                    sigmoid(L, t, lo, lo + 256)
-            for k in range(AN, 8):
-                s, half = divmod(k, 2)
-                a_turn(4 + half, s, half)
-                a_exit(s, half)
-            for s in range(NS):
-                for n in range(NN):
-                    y[s, n] = bank(order[3 * s + n], "y")
-                for G in range(NF):
-                    gate(G, s)
-                    if pend:
-                        h_quant(*pend)
-                        for n in range(NN):
-                            y_pass(pend[1], n, pend[0])
-                        if pend[0] == L:
-                            for n in range(NN):
-                                y_out(pend[1], n, False)
-                    pend = (G, s)
-            h_quant(*pend)
-            for n in range(NN):
-                y_pass(pend[1], n, pend[0])
-                y_out(pend[1], n, n == 1)
+            for lo in (0, T // 2):
+                sigmoid(NF - 1, slice(lo, lo + T // 2))
+            for s, half in COPY_A[NC]:
+                copy_a(s, half)
+            rest = [(G, s) for s in (0, 1) for G in range(NF - 1)] + [(NF - 1, 0), (NF - 1, 1)]
+            rest += [(G, s) for s in (2, 3) for G in range(NF)]
+            rest = [k for k in rest if k not in GATES.values()]
+            gate(*rest[0])
+            for i, done in enumerate(rest):
+                if i + 1 < len(rest):
+                    gate(*rest[i + 1])
+                quantize_h(*done)
+                add_to_y(*done)

from contextlib import ExitStack

import concourse.mybir as mybir
from concourse.masks import make_identity

F32 = mybir.dt.float32
BF16 = mybir.dt.bfloat16
U32 = mybir.dt.uint32
I32 = mybir.dt.int32
U8 = mybir.dt.uint8
E4M3 = mybir.dt.float8_e4m3fn
E4M3_X4 = mybir.dt.float8_e4m3fn_x4
E2M1_X4 = mybir.dt.float4_e2m1fn_x4
MULT = mybir.AluOpType.mult
COPY = mybir.ActivationFunctionType.Copy
SIGMOID = mybir.ActivationFunctionType.Sigmoid

P = 128
T, D, F = 512, 1536, 2048
FLOPS = 2 * 2 * T * D * F
SLOTS = 4
PASS = P * SLOTS
NS = T // P
NG = D // PASS
NF = F // PASS
NN = D // 512
NC = NF * NG
SCALE_BLOCK = 128
HEADS = 16

SCALAR_BLOCKS = {1: 8}
LEAD = 3

TURN_A = {4: [(2, 0)], 7: [(2, 1)], 8: [(3, 0)], 11: [(3, 1)]}
COPY_A = {2: [(0, 0), (0, 1)], 3: [(1, 0)], 6: [(1, 1), (2, 0)], 8: [(2, 1)], 10: [(3, 0)], NC: [(3, 1)]}
GATES = {7: (0, 0), 8: (1, 0)}
OUT_BANKS = ((5, 6, 7), (0, 1, 2), (3, 5, 6), (7, 0, 1))


def tile_sigmoid_gated_attention_output_d4_kernel(
    tc, X_bytes, X_scale, Wg_bytes, Wg_scale, A, Wo_words, Wo_scales, out
):
    nc = tc.nc
    with ExitStack() as ctx:
        keep = ctx.enter_context(tc.tile_pool(name="keep", bufs=1))
        stage = ctx.enter_context(tc.tile_pool(name="stage", bufs=3))
        psum = ctx.enter_context(tc.psum_pool(name="psum", bufs=1))

        def bank(i, name):
            return psum.tile([P, 512], F32, name=name, tag="bank%d" % i)

        def keep_list(count, shape, dtype, name):
            return [keep.tile(shape, dtype, name="%s%d" % (name, i), align_bytes=64) for i in range(count)]

        x_bytes = keep_list(NS, [P, D], U8, "x_bytes")
        x_values = keep_list(NS, [P, D], BF16, "x_values")
        x_words = keep_list(NG, [P, SLOTS * T], BF16, "x_words")
        x_codes = keep_list(NG, [P, T], U32, "x_codes")
        x_code_scales = keep_list(NG, [P, T], U8, "x_code_scales")
        x_scale = keep.tile([P, NS, D // SCALE_BLOCK], F32, name="x_scale", align_bytes=64)
        w_codes = keep_list(NC, [P, PASS], U32, "w_codes")
        w_code_scales = keep_list(NC, [P, PASS], U8, "w_code_scales")
        wg_scale = keep.tile([P, NG, F // SCALE_BLOCK], F32, name="wg_scale", align_bytes=64)
        a_rows = keep_list(NS, [P, F], BF16, "a_rows")
        a_turned = keep_list(NS, [P, NF, SLOTS * P], BF16, "a_turned")
        gate_values = keep_list(NF, [P, SLOTS, T], F32, "gate_values")
        h_codes = keep_list(NF, [P, T], U32, "h_codes")
        h_code_scales = keep_list(NF, [P, T], U8, "h_code_scales")
        wo_codes = keep_list(NF, [P, 2 * D], U8, "wo_codes")
        wo_code_scales = keep.tile([P, NF, D], U8, name="wo_code_scales", align_bytes=64)
        ident = keep.tile([P, P], F32, name="ident")
        warm = keep.tile([P, 2], F32, name="warm")

        nc.gpsimd.memset(warm[:], 0.0)
        make_identity(nc, ident[:])
        nc.gpsimd.memset(wo_code_scales[:].rearrange("p g n -> p (g n)").bitcast(I32), 0)

        w_bytes = {}

        def load_x_scale():
            nc.scalar.dma_start(out=x_scale[:], in_=X_scale.rearrange("(p s) j -> p s j", s=NS))

        def load_x(s):
            nc.sync.dma_start(out=x_bytes[s][:], in_=X_bytes.rearrange("(p s) k -> s p k", s=NS)[s])

        def load_w(c):
            G, g = divmod(c, NG)
            w_bytes[c] = stage.tile([P, SLOTS * 512], U8, name="w_bytes", tag="w_bytes", bufs=8, align_bytes=64)
            nc.sync.dma_start(
                out=w_bytes[c][:].rearrange("p (j n) -> p j n", j=SLOTS),
                in_=Wg_bytes[PASS * g : PASS * (g + 1), 512 * G : 512 * (G + 1)].rearrange("(p j) n -> p j n", j=SLOTS),
            )

        def load_wg_scale():
            for q in range(4):
                nc.sync.dma_start(
                    out=wg_scale[32 * q : 32 * (q + 1), :, :],
                    in_=Wg_scale.rearrange("(g q) b -> q g b", q=4)[q].partition_broadcast(32),
                )

        def load_a(s):
            nc.sync.dma_start(
                out=a_rows[s][:].rearrange("p (c e) -> p c e", c=HEADS),
                in_=A.rearrange("c (p s) e -> s p c e", s=NS)[s],
            )

        def load_wo(G):
            nc.sync.dma_start(out=wo_codes[G][:], in_=Wo_words[G])

        def load_wo_scales():
            for q in range(4):
                nc.sync.dma_start(
                    out=wo_code_scales[32 * q : 32 * q + 4, :, :].bitcast(I32),
                    in_=Wo_scales.rearrange("g (q r) n -> q r g n", r=4)[q].bitcast(I32),
                )

        x_turned = {}

        def scale_x(s):
            for j in range(D // SCALE_BLOCK):
                cols = slice(SCALE_BLOCK * j, SCALE_BLOCK * (j + 1))
                values = x_values[s][:, cols]
                codes = x_bytes[s][:, cols].bitcast(E4M3)
                if j < SCALAR_BLOCKS.get(s, 0):
                    nc.scalar.activation(out=values, in_=codes, func=COPY, scale=x_scale[:, s, j : j + 1])
                else:
                    nc.vector.tensor_scalar(
                        out=values, in0=codes, scalar1=x_scale[:, s, j : j + 1], scalar2=None, op0=MULT
                    )

        def transpose_words(dst, rows, group):
            words = rows.bitcast(F32)
            for u in range(2):
                nc.tensor.transpose(dst[u], words[:, 256 * group + u : 256 * (group + 1) : 2], ident[:])

        def turn_x(half):
            for g in range(NG):
                x_turned[half, g] = bank(NG * half + g, "x_turned")
                for i in range(2):
                    dst = [x_turned[half, g][:, 256 * u + P * i : 256 * u + P * (i + 1)] for u in range(2)]
                    transpose_words(dst, x_values[2 * half + i][:], g)

        def copy_x(half):
            for g in range(NG):
                nc.scalar.copy(
                    out=x_words[g][:, 1024 * half : 1024 * (half + 1)].bitcast(F32).rearrange("p (r u) -> p r u", u=2),
                    in_=x_turned[half, g][:].rearrange("p (u r) -> p r u", u=2),
                )

        def quantize_x(half):
            for g in range(NG):
                cols = slice(256 * half, 256 * (half + 1))
                nc.vector.quantize_mx(
                    out=x_codes[g][:, cols].bitcast(E4M3_X4),
                    scales=x_code_scales[g][:, cols],
                    in_=x_words[g][:, 1024 * half : 1024 * (half + 1)],
                )

        w_wide, w_words = {}, {}

        def widen(c):
            w_wide[c] = stage.tile([P, SLOTS * 512], BF16, name="w_wide", tag="w_wide", bufs=6, align_bytes=64)
            nc.scalar.copy(out=w_wide[c][:], in_=w_bytes[c][:].bitcast(E4M3))

        def weave(c, blocks):
            G, g = divmod(c, NG)
            if c not in w_words:
                w_words[c] = stage.tile([P, SLOTS * 512], BF16, name="w_words", tag="w_words", align_bytes=64)
            dst = w_words[c][:].rearrange("p (t m j) -> p m j t", t=SLOTS, j=SLOTS)
            src = w_wide[c][:].rearrange("p (j m t) -> p m j t", j=SLOTS, t=SLOTS)
            for b in blocks:
                rows = slice(32 * b, 32 * (b + 1))
                nc.vector.tensor_scalar(
                    out=dst[:, rows],
                    in0=src[:, rows],
                    scalar1=wg_scale[:, g, 4 * G + b : 4 * G + b + 1],
                    scalar2=None,
                    op0=MULT,
                )

        def quantize_w(c):
            nc.vector.quantize_mx(out=w_codes[c][:].bitcast(E4M3_X4), scales=w_code_scales[c][:], in_=w_words[c][:])

        z = {}

        def multiply_z(c):
            G, g = divmod(c, NG)
            for t in range(SLOTS):
                if g == 0:
                    z[G, t] = bank(t, "z")
                cols = slice(P * t, P * (t + 1))
                nc.tensor.matmul_mx(
                    out=z[G, t][:],
                    lhsT=w_codes[c][:, cols].bitcast(E4M3_X4),
                    lhsT_scale=w_code_scales[c][:, cols],
                    rhs=x_codes[g][:].bitcast(E4M3_X4),
                    rhs_scale=x_code_scales[g][:],
                    start=(g == 0),
                    stop=(g == NG - 1),
                )

        def sigmoid(G, tokens):
            for t in range(SLOTS):
                nc.scalar.activation(out=gate_values[G][:, t, tokens], in_=z[G, t][:, tokens], func=SIGMOID)

        a_banks = {}

        def turn_a(i, s, half):
            a_banks[s, half] = bank(i, "a_bank")
            for k in range(2):
                dst = [a_banks[s, half][:, 256 * k + P * u : 256 * k + P * (u + 1)] for u in range(2)]
                transpose_words(dst, a_rows[s][:], 2 * half + k)

        def copy_a(s, half):
            nc.scalar.copy(
                out=a_turned[s][:, 2 * half : 2 * half + 2, :].bitcast(F32).rearrange("p k (r u) -> p k r u", u=2),
                in_=a_banks[s, half][:].rearrange("p (k u r) -> p k r u", k=2, u=2),
            )

        h_words, y = {}, {}

        def gate(G, s):
            h_words[G, s] = stage.tile([P, SLOTS * P], BF16, name="h_words", tag="h_words", align_bytes=64)
            nc.vector.tensor_tensor(
                out=h_words[G, s][:].rearrange("p (c i t) -> p c t i", i=4, t=SLOTS),
                in0=gate_values[G][:, :, P * s : P * (s + 1)].rearrange("p t (c i) -> p c t i", i=4),
                in1=a_turned[s][:, G, :].rearrange("p (c i t) -> p c t i", i=4, t=SLOTS),
                op=MULT,
            )

        def quantize_h(G, s):
            cols = slice(P * s, P * (s + 1))
            nc.vector.quantize_mx(
                out=h_codes[G][:, cols].bitcast(E4M3_X4), scales=h_code_scales[G][:, cols], in_=h_words[G, s][:]
            )

        def multiply_y(G, s, n):
            if G == 0:
                y[s, n] = bank(OUT_BANKS[s][n], "y")
            cols = slice(P * s, P * (s + 1))
            nc.tensor.matmul_mx(
                out=y[s, n][:],
                lhsT=h_codes[G][:, cols].bitcast(E4M3_X4),
                lhsT_scale=h_code_scales[G][:, cols],
                rhs=wo_codes[G][:, 1024 * n : 1024 * (n + 1)].bitcast(E2M1_X4),
                rhs_scale=wo_code_scales[:, G, 512 * n : 512 * (n + 1)],
                start=(G == 0),
                stop=(G == NF - 1),
            )

        def store_y(s, n, pieces):
            width = 512 // pieces
            for lo in range(0, 512, width):
                y_rows = stage.tile([P, 512], F32, name="y_rows", tag="y_rows", bufs=6, align_bytes=64)
                nc.scalar.copy(out=y_rows[:, :width], in_=y[s, n][:, lo : lo + width])
                nc.sync.dma_start(
                    out=out.rearrange("(p s) n -> s p n", s=NS)[s][:, 512 * n + lo : 512 * n + lo + width],
                    in_=y_rows[:, :width],
                )

        def add_to_y(G, s):
            last_tile = s == NS - 1
            for n in range(NN - 1 if last_tile else NN):
                multiply_y(G, s, n)
                if G == NF - 1:
                    store_y(s, n, 1)
            if last_tile and G == NF - 1:
                for k in range(NF):
                    multiply_y(k, s, NN - 1)
                store_y(s, NN - 1, 2)

        with tc.manual_schedule():
            load_x_scale()
            nc.scalar.activation(out=warm[:, 1:2], in_=warm[:, 0:1], func=SIGMOID)
            load_x(1)
            load_x(0)
            load_w(0)
            load_x(3)
            load_w(1)
            load_x(2)
            load_w(2)
            load_wg_scale()
            load_a(0)
            load_w(3)
            load_w(4)
            load_a(1)
            load_w(5)
            load_w(6)
            load_w(7)
            load_a(2)
            load_w(8)
            load_w(9)
            load_wo_scales()
            load_wo(0)
            load_w(10)
            load_a(3)
            load_wo(1)
            load_w(11)
            load_wo(2)
            load_wo(3)

            scale_x(1)
            scale_x(0)
            turn_x(0)
            widen(0)
            widen(1)
            scale_x(3)
            copy_x(0)
            scale_x(2)
            turn_x(1)
            copy_x(1)
            weave(0, range(4))
            weave(1, range(4))
            turn_a(7, 0, 1)
            turn_a(6, 0, 0)
            quantize_x(0)
            quantize_w(0)
            quantize_x(1)
            quantize_w(1)
            for c in range(2, 2 + LEAD):
                widen(c)
            multiply_z(0)
            turn_a(5, 1, 1)
            turn_a(4, 1, 0)
            weave(2, range(4))
            multiply_z(1)

            for c in range(2, NC):
                G, g = divmod(c, NG)
                if g == 0:
                    sigmoid(G - 1, slice(0, T))
                if c + LEAD < NC:
                    widen(c + LEAD)
                for s, half in COPY_A.get(c, []):
                    copy_a(s, half)
                if c + 1 < NC:
                    weave(c + 1, (0, 1))
                if c in GATES:
                    gate(*GATES[c])
                quantize_w(c)
                multiply_z(c)
                for s, half in TURN_A.get(c, []):
                    turn_a(4, s, half)
                if c + 1 < NC:
                    weave(c + 1, (2, 3))
                if c in GATES:
                    quantize_h(*GATES[c])
                    add_to_y(*GATES[c])

            for lo in (0, T // 2):
                sigmoid(NF - 1, slice(lo, lo + T // 2))
            for s, half in COPY_A[NC]:
                copy_a(s, half)
            rest = [(G, s) for s in (0, 1) for G in range(NF - 1)] + [(NF - 1, 0), (NF - 1, 1)]
            rest += [(G, s) for s in (2, 3) for G in range(NF)]
            rest = [k for k in rest if k not in GATES.values()]
            gate(*rest[0])
            for i, done in enumerate(rest):
                if i + 1 < len(rest):
                    gate(*rest[i + 1])
                quantize_h(*done)
                add_to_y(*done)
